import numpy as np
import ml_dtypes


def mxq(x, axis, fmt="e4m3"):
    dtype, down = {"e4m3": (ml_dtypes.float8_e4m3fn, 7), "e5m2": (ml_dtypes.float8_e5m2, 14)}[fmt]
    v = np.moveaxis(np.asarray(x, np.float32).astype(ml_dtypes.bfloat16).astype(np.float64), axis, -1)
    blocks = v.reshape(v.shape[:-1] + (-1, 32))
    amax = np.abs(blocks).max(-1, keepdims=True)
    byte = np.maximum(np.where(amax > 0, np.frexp(amax)[1] - 1 + 127, 0) - down, 1)
    scale = np.exp2(byte - 127.0)
    codes = (blocks / scale).astype(np.float32).astype(dtype).astype(np.float64)
    return np.moveaxis((codes * scale).reshape(v.shape), -1, axis)


WIDE = False


def mx_kscale(k):
    if not WIDE:
        return np.ones(k)
    levels = np.array([30, -30])
    if k % 512:
        return np.exp2(np.random.permutation(np.resize(levels, k // 32))).repeat(32)
    a = np.empty((k // 512, 16))
    for p in range(k // 512):
        a[p, :8] = np.random.permutation(np.resize(levels, 8))
        for g in range(8):
            far = levels[np.abs(levels - a[p, g]) >= 10]
            a[p, g + 8] = far[np.random.randint(len(far))]
    return np.exp2(a.ravel()).repeat(32)


def f64(x):
    return np.asarray(x).astype(np.float64)


def striped(idx):
    return np.tile(np.asarray(idx).reshape(-1, 16).T, (8, 1)).astype(np.uint16)


def unstriped(offs):
    return offs[:16].T.reshape(-1).astype(np.int64)


E2M1 = np.array([0.0, 0.5, 1.0, 1.5, 2.0, 3.0, 4.0, 6.0, -0.0, -0.5, -1.0, -1.5, -2.0, -3.0, -4.0, -6.0])


def pack_weight(w, fmt):
    k, n = w.shape
    w = f64(np.asarray(w, np.float32).astype(ml_dtypes.bfloat16)).reshape(k // 32, 32, n)
    amax = np.abs(w).max(1)
    if fmt in ("e4m3", "e5m2"):
        byte = np.frexp(amax)[1] - 1 + 127 - (7 if fmt == "e4m3" else 14)
    else:
        mant, ex = np.frexp(amax / 6.0)
        byte = np.where(mant > 0.5, ex, ex - 1) + 127
    byte = np.clip(np.where(amax > 0, byte, 1), 1, 254)
    scaled = (w * np.exp2(127.0 - byte)[:, None, :]).reshape(k, n).astype(np.float32)
    by_word = np.ascontiguousarray(scaled.reshape(k // 512, 128, 4, n).transpose(0, 1, 3, 2))
    if fmt in ("e4m3", "e5m2"):
        words = by_word.astype(ml_dtypes.float8_e4m3fn if fmt == "e4m3" else ml_dtypes.float8_e5m2).view(np.uint8)
    else:
        c = by_word.astype(ml_dtypes.float4_e2m1fn).view(np.uint8) & 0xF
        words = (c[..., 0::2] | (c[..., 1::2] << 4)).reshape(k // 512, 128, 2 * n)
    return np.ascontiguousarray(words), np.ascontiguousarray(byte.astype(np.uint8).reshape(k // 512, 16, n))


def unpack_weight(words, scales, fmt):
    g, _, n = scales.shape
    words = np.ascontiguousarray(words).reshape(g, 128, n, -1)
    if fmt in ("e4m3", "e5m2"):
        vals = words.view(ml_dtypes.float8_e4m3fn if fmt == "e4m3" else ml_dtypes.float8_e5m2).astype(np.float64)
    else:
        nib = np.empty((g, 128, n, 4), np.uint8)
        nib[..., 0::2] = words & 0xF
        nib[..., 1::2] = words >> 4
        vals = E2M1[nib]
    vals = vals * np.repeat(np.exp2(scales.astype(np.float64) - 127.0), 8, axis=1)[..., None]
    return vals.transpose(0, 1, 3, 2).reshape(g * 512, n)


K, T, J, R, F, Z, X, V, O, N, E = 512, 1024, 256, 512, 512, 1024, 512, 512, 128, 256, 512


def setup_inputs():
    n = np.random.standard_normal
    idx = np.random.permutation(T)[:J]
    idx2 = np.random.permutation(Z)[:J]
    idx3 = np.random.permutation(X)[:O]
    idx4 = np.random.permutation(V)[:O]
    idx5 = np.random.permutation(J)[:O]
    idx6 = np.random.permutation(E)[:O]
    idx7 = np.random.permutation(E)[:O]
    fk = mx_kscale(K)
    ff = mx_kscale(F)
    fr = mx_kscale(R)
    xtp = pack_weight(n((K, T)) / fk[:, None], "e2m1")
    xop = pack_weight(n((F, Z)) / ff[:, None], "e5m2")
    wp = pack_weight(n((K, R)) * 1 / np.sqrt(K) * fk[:, None] * fr, "e5m2")
    w0p = pack_weight(n((F, R)) * 1 / np.sqrt(F) * ff[:, None] * fr, "e4m3")
    wbp = pack_weight(n((R, N)) * 1 / np.sqrt(R) / fr[:, None], "e4m3")
    return {
        "xt_words": xtp[0],
        "xt_scales": xtp[1],
        "xo_words": xop[0],
        "xo_scales": xop[1],
        "w_words": wp[0],
        "w_scales": wp[1],
        "w0_words": w0p[0],
        "w0_scales": w0p[1],
        "tb": (n((R, X)) * 0.9).astype(np.float32),
        "tc2": (n((R, V)) * 0.9).astype(np.float32),
        "wb_words": wbp[0],
        "wb_scales": wbp[1],
        "offs": striped(idx),
        "offs2": striped(idx2),
        "offs3": striped(idx3),
        "offs4": striped(idx4),
        "offs5": striped(idx5),
        "offs6": striped(idx6),
        "offs7": striped(idx7),
    }


def reference(xt_words, xt_scales, xo_words, xo_scales, w_words, w_scales, w0_words, w0_scales, tb, tc2, wb_words, wb_scales, offs, offs2, offs3, offs4, offs5, offs6, offs7):
    idx = unstriped(offs)
    idx2 = unstriped(offs2)
    idx3 = unstriped(offs3)
    idx4 = unstriped(offs4)
    idx5 = unstriped(offs5)
    idx6 = unstriped(offs6)
    idx7 = unstriped(offs7)
    xtu = unpack_weight(xt_words, xt_scales, "e2m1")
    xou = unpack_weight(xo_words, xo_scales, "e5m2")
    wu = unpack_weight(w_words, w_scales, "e5m2")
    w0u = unpack_weight(w0_words, w0_scales, "e4m3")
    wbu = unpack_weight(wb_words, wb_scales, "e4m3")
    xtidxg = xtu[:, idx]
    xoidx2g = xou[:, idx2]
    a = wu.T @ xtidxg + w0u.T @ xoidx2g
    la = a[:, 0:1]
    la2 = a[:, 128:129]
    hid = np.maximum(f64(tb)[:, idx3] * la, f64(tc2)[:, idx4] * la2) - a[:, idx5]
    hidq = mxq(hid, 0, "e5m2")
    p = wbu.T @ hidq
    pa = np.zeros((N, E))
    pa[:, idx6] = p
    pb = np.zeros((N, E))
    pb[:, idx7] = p
    y = pa + pb
    return y

@@ -1,0 +1,192 @@
+from contextlib import ExitStack
+
+import concourse.mybir as mybir
+
+FLOPS = 301989888
+
+F32 = mybir.dt.float32
+BF16 = mybir.dt.bfloat16
+I32 = mybir.dt.int32
+U32 = mybir.dt.uint32
+U16 = mybir.dt.uint16
+U8 = mybir.dt.uint8
+E4M3 = mybir.dt.float8_e4m3fn_x4
+E5M2 = mybir.dt.float8_e5m2_x4
+E2M1 = mybir.dt.float4_e2m1fn_x4
+COPY = mybir.ActivationFunctionType.Copy
+ALU = mybir.AluOpType
+
+P = 128
+PACK = 4
+QUADS = 4
+T, J, R, X, O, N, E = 1024, 256, 512, 512, 128, 256, 512
+HALF = J // 2
+
+
+def tile_list_twotables_bank_one_pagetwice_kernel(
+    tc, xt_words, xt_scales, xo_words, xo_scales, w_words, w_scales, w0_words, w0_scales,
+    tb, tc2, wb_words, wb_scales, offs, offs2, offs3, offs4, offs5, offs6, offs7, out,
+):
+    nc = tc.nc
+    with ExitStack() as ctx:
+        sb = ctx.enter_context(tc.tile_pool(name="sb", bufs=1))
+        ps = ctx.enter_context(tc.psum_pool(name="ps", bufs=1))
+
+        def load_list(name, dram):
+            tile = sb.tile(list(dram.shape), U16, name=name)
+            nc.sync.dma_start(tile[:], dram)
+            return tile
+
+        def load_words(name, dram_bytes, dtype, columns):
+            tile = sb.tile([P, columns], dtype, name=name, align_bytes=64)
+            nc.sync.dma_start(tile[:].bitcast(I32), dram_bytes.bitcast(I32))
+            return tile
+
+        def by_quadrant(scales):
+            return scales[0].bitcast(I32).rearrange("(q r) c -> r q c", r=PACK)
+
+        def load_rows(name, dram, t):
+            tile = sb.tile([P, X], F32, name=name)
+            nc.sync.dma_start(tile[:], dram.rearrange("(p t) x -> t p x", t=PACK)[t])
+            return tile
+
+        l1 = load_list("l1", offs)
+        xt_stage = sb.tile([PACK, QUADS, T // 4], I32, name="xt_stage")
+        nc.sync.dma_start(xt_stage[:], by_quadrant(xt_scales))
+        w_stage = sb.tile([PACK, QUADS, 2, R // 4], I32, name="w_stage")
+        nc.sync.dma_start(w_stage[:, :, 0, :], by_quadrant(w_scales))
+        nc.sync.dma_start(w_stage[:, :, 1, :], by_quadrant(w0_scales))
+        xt_w = load_words("xt_w", xt_words[0], U16, T)
+        w_raw = load_words("w_raw", w_words[0].rearrange("p n t -> p (n t)"), U32, R)
+        w0_raw = load_words("w0_raw", w0_words[0].rearrange("p n t -> p (n t)"), U32, R)
+        xo_w = load_words("xo_w", xo_words[0].rearrange("p n t -> p (n t)"), U32, T)
+        xo_stage = sb.tile([PACK, QUADS, T // 4], I32, name="xo_stage")
+        nc.sync.dma_start(xo_stage[:], by_quadrant(xo_scales))
+        l2 = load_list("l2", offs2)
+        tb_t = [load_rows("tb%d" % t, tb, t) for t in range(2)]
+        l3 = load_list("l3", offs3)
+        tb_t.extend(load_rows("tb%d" % t, tb, t) for t in range(2, PACK))
+        l4 = load_list("l4", offs4)
+        l5 = load_list("l5", offs5)
+        tc_t = [load_rows("tc%d" % t, tc2, t) for t in range(PACK)]
+        wb_w = load_words("wb_w", wb_words[0].rearrange("p n t -> p (n t)"), U32, N)
+        wb_stage = sb.tile([PACK, QUADS, N // 4], I32, name="wb_stage")
+        nc.sync.dma_start(wb_stage[:], by_quadrant(wb_scales))
+        l6 = load_list("l6", offs6)
+        l7 = load_list("l7", offs7)
+
+        wb_s = sb.tile([P, N], U8, name="wb_s", align_bytes=64)
+
+        xt_s = sb.tile([P, T], U8, name="xt_s")
+        xo_s = sb.tile([P, T], U8, name="xo_s")
+        ws_raw = sb.tile([P, 2 * R], U8, name="ws_raw")
+        for tile in (xt_s, xo_s, ws_raw, wb_s):
+            nc.vector.memset(tile[:].bitcast(I32), 0)
+        pa = [sb.tile([P, E], F32, name="pa%d" % h) for h in range(2)]
+        pb = [sb.tile([P, E], F32, name="pb%d" % h) for h in range(2)]
+        for tile in pa + pb:
+            nc.vector.memset(tile[:], 0.0)
+
+        def spread(plane, stage_of):
+            for q in range(QUADS):
+                nc.vector.tensor_copy(plane[32 * q : 32 * q + PACK, :].bitcast(I32), stage_of(q))
+
+        spread(xt_s, lambda q: xt_stage[:, q, :])
+
+        w_p = sb.tile([P, R], U32, name="w_p", align_bytes=64)
+        w0_p = sb.tile([P, R], U32, name="w0_p", align_bytes=64)
+        for dealt, raw in ((w_p, w_raw), (w0_p, w0_raw)):
+            nc.scalar.copy(dealt[:].rearrange("p (t m) -> p m t", t=PACK), raw[:].rearrange("p (m t) -> p m t", t=PACK))
+
+        def gather(name, window, offsets, dtype):
+            tile = sb.tile([P, HALF], dtype, name=name, align_bytes=64)
+            nc.vector.tensor_copy(tile[:], window[:].indirect(offsets))
+            return tile
+
+        def half(tile, h):
+            return tile[:, 8 * h : 8 * (h + 1)]
+
+        xt_gs0 = gather("xt_gs0", xt_s, half(l1, 0), U8)
+        xt_gw0 = gather("xt_gw0", xt_w, half(l1, 0), U16)
+
+        spread(ws_raw, lambda q: w_stage[:, q, :, :].rearrange("p i c -> p (i c)"))
+        ws_p = sb.tile([P, 2 * R], U8, name="ws_p", align_bytes=64)
+        nc.vector.tensor_copy(
+            ws_p[:].rearrange("p (i t m) -> p i m t", i=2, t=PACK), ws_raw[:].rearrange("p (i m t) -> p i m t", i=2, t=PACK)
+        )
+
+        spread(xo_s, lambda q: xo_stage[:, q, :])
+
+        a_sb = sb.tile([P, PACK, J], F32, name="a_sb")
+
+        def first_stage(h, xt_gw, xt_gs):
+            xo_gs = gather("xo_gs%d" % h, xo_s, half(l2, h), U8)
+            xo_gw = gather("xo_gw%d" % h, xo_w, half(l2, h), U32)
+            bank = ps.tile([P, PACK, HALF], F32, name="a_ps%d" % h)
+            for t in range(PACK):
+                cols = slice(P * t, P * (t + 1))
+                nc.tensor.matmul_mx(
+                    bank[:, t, :], lhsT=w_p[:, cols].bitcast(E5M2), lhsT_scale=ws_p[:, cols],
+                    rhs=xt_gw[:].bitcast(E2M1), rhs_scale=xt_gs[:], start=(t == 0), stop=False,
+                )
+            for t in range(PACK):
+                cols = slice(P * t, P * (t + 1))
+                nc.tensor.matmul_mx(
+                    bank[:, t, :], lhsT=w0_p[:, cols].bitcast(E4M3), lhsT_scale=ws_p[:, R + P * t : R + P * (t + 1)],
+                    rhs=xo_gw[:].bitcast(E5M2), rhs_scale=xo_gs[:], start=False, stop=(t == PACK - 1),
+                )
+            return bank
+
+        def look(name, table, offsets, scale):
+            tile = sb.tile([P, O], F32, name=name)
+            nc.scalar.activation(tile[:], table[:].indirect(offsets[:]), COPY, scale=scale)
+            return tile
+
+        bank0 = first_stage(0, xt_gw0, xt_gs0)
+        nc.scalar.copy(a_sb[:, :, 0:HALF], bank0[:])
+        xt_gs1 = gather("xt_gs1", xt_s, half(l1, 1), U8)
+        xt_gw1 = gather("xt_gw1", xt_w, half(l1, 1), U16)
+        bank1 = first_stage(1, xt_gw1, xt_gs1)
+        g1 = [look("g1_%d" % t, tb_t[t], l3, a_sb[:, t, 0:1]) for t in range(PACK)]
+        nc.vector.tensor_copy(a_sb[:, :, HALF:J], bank1[:])
+        spread(wb_s, lambda q: wb_stage[:, q, :])
+
+        a_g = sb.tile([P, PACK, O], F32, name="a_g")
+        top = sb.tile([P, PACK, O], F32, name="top")
+        hid = sb.tile([P, O, PACK], BF16, name="hid", align_bytes=64)
+        for pair in range(2):
+            ts = slice(2 * pair, 2 * pair + 2)
+            for t in range(ts.start, ts.stop):
+                nc.vector.tensor_copy(a_g[:, t, :], a_sb[:, t, :].indirect(l5[:]))
+            for t in range(ts.start, ts.stop):
+                g2 = look("g2_%d" % t, tc_t[t], l4, a_sb[:, t, HALF : HALF + 1])
+                nc.vector.tensor_tensor(top[:, t, :], g1[t][:], g2[:], ALU.max)
+            nc.vector.tensor_tensor(
+                hid[:, :, ts], top[:, ts, :].rearrange("p t o -> p o t"), a_g[:, ts, :].rearrange("p t o -> p o t"), ALU.subtract
+            )
+
+        hid_w = sb.tile([P, O], U32, name="hid_w", align_bytes=64)
+        hid_s = sb.tile([P, O], U8, name="hid_s", align_bytes=64)
+        nc.vector.quantize_mx(hid_w[:].bitcast(E5M2), hid_s[:], hid[:].rearrange("p o t -> p (o t)"))
+
+        p_sb = []
+        for h in range(2):
+            cols = slice(P * h, P * (h + 1))
+            bank = ps.tile([P, O], F32, name="p_ps%d" % h)
+            nc.tensor.matmul_mx(
+                bank[:], lhsT=wb_w[:, cols].bitcast(E4M3), lhsT_scale=wb_s[:, cols],
+                rhs=hid_w[:].bitcast(E5M2), rhs_scale=hid_s[:], start=True, stop=True,
+            )
+            tile = sb.tile([P, O], F32, name="p_sb%d" % h)
+            if h == 0:
+                nc.vector.tensor_copy(tile[:], bank[:])
+            else:
+                nc.scalar.copy(tile[:], bank[:])
+            p_sb.append(tile)
+        for h in range(2):
+            nc.vector.tensor_copy(pa[h][:].indirect(l6[:]), p_sb[h][:])
+            nc.scalar.activation(pb[h][:].indirect(l7[:]), p_sb[h][:], COPY)
+        for h in range(2):
+            total = sb.tile([P, E], F32, name="total%d" % h)
+            nc.vector.tensor_tensor(total[:], pa[h][:], pb[h][:], ALU.add)
+            nc.sync.dma_start(out[P * h : P * (h + 1), :], total[:])

@@ -50,6 +50,24 @@ def tile_list_twotables_bank_one_pagetwice_kernel(
             nc.sync.dma_start(tile[:], dram.rearrange("(p t) x -> t p x", t=PACK)[t])
             return tile
 
+        def load_plane(plane, scales):
+            for q in range(QUADS):
+                nc.sync.dma_start(
+                    plane[32 * q : 32 * q + PACK, :].bitcast(I32), scales[0, PACK * q : PACK * (q + 1), :].bitcast(I32)
+                )
+
+        xt_s = sb.tile([P, T], U8, name="xt_s")
+        xo_s = sb.tile([P, T], U8, name="xo_s")
+        ws_raw = sb.tile([P, 2 * R], U8, name="ws_raw")
+        wb_s = sb.tile([P, N], U8, name="wb_s", align_bytes=64)
+        nc.gpsimd.memset(xo_s[:].bitcast(I32), 0)
+        for tile in (xt_s, ws_raw, wb_s):
+            nc.vector.memset(tile[:].bitcast(I32), 0)
+        pa = [sb.tile([P, E], F32, name="pa%d" % h) for h in range(2)]
+        pb = [sb.tile([P, E], F32, name="pb%d" % h) for h in range(2)]
+        for tile in pa + pb:
+            nc.gpsimd.memset(tile[:], 0.0)
+
         l1 = load_list("l1", offs)
         xt_stage = sb.tile([PACK, QUADS, T // 4], I32, name="xt_stage")
         nc.sync.dma_start(xt_stage[:], by_quadrant(xt_scales))
@@ -60,8 +78,7 @@ def tile_list_twotables_bank_one_pagetwice_kernel(
         w_raw = load_words("w_raw", w_words[0].rearrange("p n t -> p (n t)"), U32, R)
         w0_raw = load_words("w0_raw", w0_words[0].rearrange("p n t -> p (n t)"), U32, R)
         xo_w = load_words("xo_w", xo_words[0].rearrange("p n t -> p (n t)"), U32, T)
-        xo_stage = sb.tile([PACK, QUADS, T // 4], I32, name="xo_stage")
-        nc.sync.dma_start(xo_stage[:], by_quadrant(xo_scales))
+        load_plane(xo_s, xo_scales)
         l2 = load_list("l2", offs2)
         tb_t = [load_rows("tb%d" % t, tb, t) for t in range(2)]
         l3 = load_list("l3", offs3)
@@ -70,22 +87,9 @@ def tile_list_twotables_bank_one_pagetwice_kernel(
         l5 = load_list("l5", offs5)
         tc_t = [load_rows("tc%d" % t, tc2, t) for t in range(PACK)]
         wb_w = load_words("wb_w", wb_words[0].rearrange("p n t -> p (n t)"), U32, N)
-        wb_stage = sb.tile([PACK, QUADS, N // 4], I32, name="wb_stage")
-        nc.sync.dma_start(wb_stage[:], by_quadrant(wb_scales))
         l6 = load_list("l6", offs6)
         l7 = load_list("l7", offs7)
-
-        wb_s = sb.tile([P, N], U8, name="wb_s", align_bytes=64)
-
-        xt_s = sb.tile([P, T], U8, name="xt_s")
-        xo_s = sb.tile([P, T], U8, name="xo_s")
-        ws_raw = sb.tile([P, 2 * R], U8, name="ws_raw")
-        for tile in (xt_s, xo_s, ws_raw, wb_s):
-            nc.vector.memset(tile[:].bitcast(I32), 0)
-        pa = [sb.tile([P, E], F32, name="pa%d" % h) for h in range(2)]
-        pb = [sb.tile([P, E], F32, name="pb%d" % h) for h in range(2)]
-        for tile in pa + pb:
-            nc.vector.memset(tile[:], 0.0)
+        load_plane(wb_s, wb_scales)
 
         def spread(plane, stage_of):
             for q in range(QUADS):
@@ -96,7 +100,9 @@ def tile_list_twotables_bank_one_pagetwice_kernel(
         w_p = sb.tile([P, R], U32, name="w_p", align_bytes=64)
         w0_p = sb.tile([P, R], U32, name="w0_p", align_bytes=64)
         for dealt, raw in ((w_p, w_raw), (w0_p, w0_raw)):
-            nc.scalar.copy(dealt[:].rearrange("p (t m) -> p m t", t=PACK), raw[:].rearrange("p (m t) -> p m t", t=PACK))
+            nc.scalar.copy(
+                dealt[:].rearrange("p (t c m) -> p c t m", t=PACK, m=4), raw[:].rearrange("p (c m t) -> p c t m", t=PACK, m=4)
+            )
 
         def gather(name, window, offsets, dtype):
             tile = sb.tile([P, HALF], dtype, name=name, align_bytes=64)
@@ -112,10 +118,8 @@ def tile_list_twotables_bank_one_pagetwice_kernel(
         spread(ws_raw, lambda q: w_stage[:, q, :, :].rearrange("p i c -> p (i c)"))
         ws_p = sb.tile([P, 2 * R], U8, name="ws_p", align_bytes=64)
         nc.vector.tensor_copy(
-            ws_p[:].rearrange("p (i t m) -> p i m t", i=2, t=PACK), ws_raw[:].rearrange("p (i m t) -> p i m t", i=2, t=PACK)
+            ws_p[:].rearrange("p (i t m) -> p i t m", i=2, t=PACK), ws_raw[:].rearrange("p (i m t) -> p i t m", i=2, t=PACK)
         )
-
-        spread(xo_s, lambda q: xo_stage[:, q, :])
 
         a_sb = sb.tile([P, PACK, J], F32, name="a_sb")
 
@@ -137,33 +141,44 @@ def tile_list_twotables_bank_one_pagetwice_kernel(
                 )
             return bank
 
-        def look(name, table, offsets, scale):
-            tile = sb.tile([P, O], F32, name=name)
-            nc.scalar.activation(tile[:], table[:].indirect(offsets[:]), COPY, scale=scale)
-            return tile
+        def look(product, table, offsets, scale):
+            nc.scalar.activation(product, table[:].indirect(offsets[:]), COPY, scale=scale)
 
-        bank0 = first_stage(0, xt_gw0, xt_gs0)
-        nc.scalar.copy(a_sb[:, :, 0:HALF], bank0[:])
-        xt_gs1 = gather("xt_gs1", xt_s, half(l1, 1), U8)
-        xt_gw1 = gather("xt_gw1", xt_w, half(l1, 1), U16)
-        bank1 = first_stage(1, xt_gw1, xt_gs1)
-        g1 = [look("g1_%d" % t, tb_t[t], l3, a_sb[:, t, 0:1]) for t in range(PACK)]
-        nc.vector.tensor_copy(a_sb[:, :, HALF:J], bank1[:])
-        spread(wb_s, lambda q: wb_stage[:, q, :])
-
+        g1 = sb.tile([P, PACK, O], F32, name="g1")
+        g2 = sb.tile([P, PACK, O], F32, name="g2")
         a_g = sb.tile([P, PACK, O], F32, name="a_g")
         top = sb.tile([P, PACK, O], F32, name="top")
         hid = sb.tile([P, O, PACK], BF16, name="hid", align_bytes=64)
-        for pair in range(2):
-            ts = slice(2 * pair, 2 * pair + 2)
-            for t in range(ts.start, ts.stop):
-                nc.vector.tensor_copy(a_g[:, t, :], a_sb[:, t, :].indirect(l5[:]))
-            for t in range(ts.start, ts.stop):
-                g2 = look("g2_%d" % t, tc_t[t], l4, a_sb[:, t, HALF : HALF + 1])
-                nc.vector.tensor_tensor(top[:, t, :], g1[t][:], g2[:], ALU.max)
+
+        bank0 = first_stage(0, xt_gw0, xt_gs0)
+        nc.scalar.copy(a_sb[:, :, 0:HALF], bank0[:])
+        la = sb.tile([P, PACK, 1], F32, name="la")
+        nc.scalar.copy(la[:], a_sb[:, :, 0:1])
+        xt_gs1 = gather("xt_gs1", xt_s, half(l1, 1), U8)
+        xt_gw1 = gather("xt_gw1", xt_w, half(l1, 1), U16)
+        bank1 = first_stage(1, xt_gw1, xt_gs1)
+        for t in range(PACK):
+            look(g1[:, t, :], tb_t[t], l3, la[:, t, :])
+        nc.vector.tensor_copy(a_sb[:, :, HALF:J], bank1[:])
+        for t in range(PACK - 1):
+            nc.vector.tensor_copy(a_g[:, t, :], a_sb[:, t, :].indirect(l5[:]))
+        nc.scalar.activation(a_g[:, PACK - 1, :], a_sb[:, PACK - 1, :].indirect(l5[:]), COPY)
+        for t in range(PACK):
+            look(g2[:, t, :], tc_t[t], l4, a_sb[:, t, HALF : HALF + 1])
+
+        def larger(ts):
+            nc.vector.tensor_tensor(top[:, ts, :], g1[:, ts, :], g2[:, ts, :], ALU.max)
+
+        def take_off(ts):
             nc.vector.tensor_tensor(
                 hid[:, :, ts], top[:, ts, :].rearrange("p t o -> p o t"), a_g[:, ts, :].rearrange("p t o -> p o t"), ALU.subtract
             )
+
+        larger(slice(0, 2))
+        take_off(slice(0, 2))
+        larger(slice(2, 3))
+        larger(slice(3, 4))
+        take_off(slice(2, 4))
 
         hid_w = sb.tile([P, O], U32, name="hid_w", align_bytes=64)
         hid_s = sb.tile([P, O], U8, name="hid_s", align_bytes=64)

@@ -50,17 +50,12 @@ def tile_list_twotables_bank_one_pagetwice_kernel(
             nc.sync.dma_start(tile[:], dram.rearrange("(p t) x -> t p x", t=PACK)[t])
             return tile
 
-        def load_plane(plane, scales):
-            for q in range(QUADS):
-                nc.sync.dma_start(
-                    plane[32 * q : 32 * q + PACK, :].bitcast(I32), scales[0, PACK * q : PACK * (q + 1), :].bitcast(I32)
-                )
-
         xt_s = sb.tile([P, T], U8, name="xt_s")
         xo_s = sb.tile([P, T], U8, name="xo_s")
         ws_raw = sb.tile([P, 2 * R], U8, name="ws_raw")
         wb_s = sb.tile([P, N], U8, name="wb_s", align_bytes=64)
-        nc.gpsimd.memset(xo_s[:].bitcast(I32), 0)
+        xo_stage = sb.tile([P, 2, T // 4], I32, name="xo_stage")
+        nc.gpsimd.memset(xo_stage[64:P], 0)
         for tile in (xt_s, ws_raw, wb_s):
             nc.vector.memset(tile[:].bitcast(I32), 0)
         pa = [sb.tile([P, E], F32, name="pa%d" % h) for h in range(2)]
@@ -78,18 +73,23 @@ def tile_list_twotables_bank_one_pagetwice_kernel(
         w_raw = load_words("w_raw", w_words[0].rearrange("p n t -> p (n t)"), U32, R)
         w0_raw = load_words("w0_raw", w0_words[0].rearrange("p n t -> p (n t)"), U32, R)
         xo_w = load_words("xo_w", xo_words[0].rearrange("p n t -> p (n t)"), U32, T)
-        load_plane(xo_s, xo_scales)
+        xo_rows = xo_scales[0].bitcast(I32).rearrange("(s b r) c -> b r s c", s=2, r=PACK)
+        for b in range(2):
+            nc.sync.dma_start(xo_stage[64 + 32 * b : 64 + 32 * b + PACK], xo_rows[b])
         l2 = load_list("l2", offs2)
-        tb_t = [load_rows("tb%d" % t, tb, t) for t in range(2)]
+        tb_t = [load_rows("tb0", tb, 0)]
         l3 = load_list("l3", offs3)
-        tb_t.extend(load_rows("tb%d" % t, tb, t) for t in range(2, PACK))
-        l4 = load_list("l4", offs4)
+        tb_t.extend(load_rows("tb%d" % t, tb, t) for t in range(1, PACK))
         l5 = load_list("l5", offs5)
+        l4 = load_list("l4", offs4)
         tc_t = [load_rows("tc%d" % t, tc2, t) for t in range(PACK)]
         wb_w = load_words("wb_w", wb_words[0].rearrange("p n t -> p (n t)"), U32, N)
+        for q in range(QUADS):
+            nc.sync.dma_start(
+                wb_s[32 * q : 32 * q + PACK, :].bitcast(I32), wb_scales[0, PACK * q : PACK * (q + 1), :].bitcast(I32)
+            )
         l6 = load_list("l6", offs6)
         l7 = load_list("l7", offs7)
-        load_plane(wb_s, wb_scales)
 
         def spread(plane, stage_of):
             for q in range(QUADS):
@@ -121,25 +121,29 @@ def tile_list_twotables_bank_one_pagetwice_kernel(
             ws_p[:].rearrange("p (i t m) -> p i t m", i=2, t=PACK), ws_raw[:].rearrange("p (i m t) -> p i t m", i=2, t=PACK)
         )
 
-        a_sb = sb.tile([P, PACK, J], F32, name="a_sb")
+        for s in range(2):
+            nc.vector.tensor_copy(xo_s[64 * s : 64 * (s + 1), :].bitcast(I32), xo_stage[64:P, s, :])
+
+        a_t = [sb.tile([P, J], F32, name="a%d" % t) for t in range(PACK)]
 
         def first_stage(h, xt_gw, xt_gs):
-            xo_gs = gather("xo_gs%d" % h, xo_s, half(l2, h), U8)
             xo_gw = gather("xo_gw%d" % h, xo_w, half(l2, h), U32)
-            bank = ps.tile([P, PACK, HALF], F32, name="a_ps%d" % h)
+            xo_gs = gather("xo_gs%d" % h, xo_s, half(l2, h), U8)
+            banks = [ps.tile([P, 2, HALF], F32, name="a_ps%d%d" % (h, b)) for b in range(2)]
             for t in range(PACK):
                 cols = slice(P * t, P * (t + 1))
                 nc.tensor.matmul_mx(
-                    bank[:, t, :], lhsT=w_p[:, cols].bitcast(E5M2), lhsT_scale=ws_p[:, cols],
-                    rhs=xt_gw[:].bitcast(E2M1), rhs_scale=xt_gs[:], start=(t == 0), stop=False,
+                    banks[t // 2][:, t % 2, :], lhsT=w_p[:, cols].bitcast(E5M2), lhsT_scale=ws_p[:, cols],
+                    rhs=xt_gw[:].bitcast(E2M1), rhs_scale=xt_gs[:], start=(t % 2 == 0), stop=False,
                 )
             for t in range(PACK):
                 cols = slice(P * t, P * (t + 1))
                 nc.tensor.matmul_mx(
-                    bank[:, t, :], lhsT=w0_p[:, cols].bitcast(E4M3), lhsT_scale=ws_p[:, R + P * t : R + P * (t + 1)],
-                    rhs=xo_gw[:].bitcast(E5M2), rhs_scale=xo_gs[:], start=False, stop=(t == PACK - 1),
+                    banks[t // 2][:, t % 2, :], lhsT=w0_p[:, cols].bitcast(E4M3),
+                    lhsT_scale=ws_p[:, R + P * t : R + P * (t + 1)],
+                    rhs=xo_gw[:].bitcast(E5M2), rhs_scale=xo_gs[:], start=False, stop=(t % 2 == 1),
                 )
-            return bank
+            return [banks[t // 2][:, t % 2, :] for t in range(PACK)]
 
         def look(product, table, offsets, scale):
             nc.scalar.activation(product, table[:].indirect(offsets[:]), COPY, scale=scale)
@@ -150,35 +154,32 @@ def tile_list_twotables_bank_one_pagetwice_kernel(
         top = sb.tile([P, PACK, O], F32, name="top")
         hid = sb.tile([P, O, PACK], BF16, name="hid", align_bytes=64)
 
-        bank0 = first_stage(0, xt_gw0, xt_gs0)
-        nc.scalar.copy(a_sb[:, :, 0:HALF], bank0[:])
-        la = sb.tile([P, PACK, 1], F32, name="la")
-        nc.scalar.copy(la[:], a_sb[:, :, 0:1])
+        sums0 = first_stage(0, xt_gw0, xt_gs0)
         xt_gs1 = gather("xt_gs1", xt_s, half(l1, 1), U8)
         xt_gw1 = gather("xt_gw1", xt_w, half(l1, 1), U16)
-        bank1 = first_stage(1, xt_gw1, xt_gs1)
+        sums1 = first_stage(1, xt_gw1, xt_gs1)
         for t in range(PACK):
-            look(g1[:, t, :], tb_t[t], l3, la[:, t, :])
-        nc.vector.tensor_copy(a_sb[:, :, HALF:J], bank1[:])
-        for t in range(PACK - 1):
-            nc.vector.tensor_copy(a_g[:, t, :], a_sb[:, t, :].indirect(l5[:]))
-        nc.scalar.activation(a_g[:, PACK - 1, :], a_sb[:, PACK - 1, :].indirect(l5[:]), COPY)
+            nc.scalar.copy(a_t[t][:, 0:HALF], sums0[t])
+            look(g1[:, t, :], tb_t[t], l3, a_t[t][:, 0:1])
         for t in range(PACK):
-            look(g2[:, t, :], tc_t[t], l4, a_sb[:, t, HALF : HALF + 1])
+            nc.vector.tensor_copy(a_t[t][:, HALF:J], sums1[t])
+        for t in range(PACK):
+            nc.vector.tensor_copy(a_g[:, t, :], a_t[t][:].indirect(l5[:]))
+        for t in range(PACK):
+            look(g2[:, t, :], tc_t[t], l4, a_t[t][:, HALF : HALF + 1])
 
         def larger(ts):
             nc.vector.tensor_tensor(top[:, ts, :], g1[:, ts, :], g2[:, ts, :], ALU.max)
 
-        def take_off(ts):
-            nc.vector.tensor_tensor(
-                hid[:, :, ts], top[:, ts, :].rearrange("p t o -> p o t"), a_g[:, ts, :].rearrange("p t o -> p o t"), ALU.subtract
-            )
-
         larger(slice(0, 2))
-        take_off(slice(0, 2))
         larger(slice(2, 3))
         larger(slice(3, 4))
-        take_off(slice(2, 4))
+        nc.vector.tensor_tensor(
+            hid[:].rearrange("p (c i) t -> p c t i", i=4),
+            top[:].rearrange("p t (c i) -> p c t i", i=4),
+            a_g[:].rearrange("p t (c i) -> p c t i", i=4),
+            ALU.subtract,
+        )
 
         hid_w = sb.tile([P, O], U32, name="hid_w", align_bytes=64)
         hid_s = sb.tile([P, O], U8, name="hid_s", align_bytes=64)

@@ -58,10 +58,6 @@ def tile_list_twotables_bank_one_pagetwice_kernel(
         nc.gpsimd.memset(xo_stage[64:P], 0)
         for tile in (xt_s, ws_raw, wb_s):
             nc.vector.memset(tile[:].bitcast(I32), 0)
-        pa = [sb.tile([P, E], F32, name="pa%d" % h) for h in range(2)]
-        pb = [sb.tile([P, E], F32, name="pb%d" % h) for h in range(2)]
-        for tile in pa + pb:
-            nc.gpsimd.memset(tile[:], 0.0)
 
         l1 = load_list("l1", offs)
         xt_stage = sb.tile([PACK, QUADS, T // 4], I32, name="xt_stage")
@@ -181,6 +177,11 @@ def tile_list_twotables_bank_one_pagetwice_kernel(
             ALU.subtract,
         )
 
+        pa = [sb.tile([P, E], F32, name="pa%d" % h, tag=("ws_p", "xo_w")[h], align_bytes=64) for h in range(2)]
+        pb = [sb.tile([P, E], F32, name="pb%d" % h, tag=("w_p", "w0_p")[h], align_bytes=64) for h in range(2)]
+        for tile in pa + pb:
+            nc.gpsimd.memset(tile[:], 0.0)
+
         hid_w = sb.tile([P, O], U32, name="hid_w", align_bytes=64)
         hid_s = sb.tile([P, O], U8, name="hid_s", align_bytes=64)
         nc.vector.quantize_mx(hid_w[:].bitcast(E5M2), hid_s[:], hid[:].rearrange("p o t -> p (o t)"))
@@ -202,7 +203,8 @@ def tile_list_twotables_bank_one_pagetwice_kernel(
         for h in range(2):
             nc.vector.tensor_copy(pa[h][:].indirect(l6[:]), p_sb[h][:])
             nc.scalar.activation(pb[h][:].indirect(l7[:]), p_sb[h][:], COPY)
-        for h in range(2):
+        for h, cuts in enumerate(((0, E), (0, E // 2, E))):
             total = sb.tile([P, E], F32, name="total%d" % h)
-            nc.vector.tensor_tensor(total[:], pa[h][:], pb[h][:], ALU.add)
-            nc.sync.dma_start(out[P * h : P * (h + 1), :], total[:])
+            for lo, hi in zip(cuts, cuts[1:]):
+                nc.vector.tensor_tensor(total[:, lo:hi], pa[h][:, lo:hi], pb[h][:, lo:hi], ALU.add)
+                nc.sync.dma_start(out[P * h : P * (h + 1), lo:hi], total[:, lo:hi])

@@ -52,7 +52,7 @@ def tile_list_twotables_bank_one_pagetwice_kernel(
 
         xt_s = sb.tile([P, T], U8, name="xt_s")
         xo_s = sb.tile([P, T], U8, name="xo_s")
-        ws_raw = sb.tile([P, 2 * R], U8, name="ws_raw")
+        ws_raw = sb.tile([P, 2 * R], U8, name="ws_raw", align_bytes=64)
         wb_s = sb.tile([P, N], U8, name="wb_s", align_bytes=64)
         xo_stage = sb.tile([P, 2, T // 4], I32, name="xo_stage")
         nc.gpsimd.memset(xo_stage[64:P], 0)
@@ -62,7 +62,7 @@ def tile_list_twotables_bank_one_pagetwice_kernel(
         l1 = load_list("l1", offs)
         xt_stage = sb.tile([PACK, QUADS, T // 4], I32, name="xt_stage")
         nc.sync.dma_start(xt_stage[:], by_quadrant(xt_scales))
-        w_stage = sb.tile([PACK, QUADS, 2, R // 4], I32, name="w_stage")
+        w_stage = sb.tile([PACK, QUADS, 2, R // 4], I32, name="w_stage", align_bytes=64)
         nc.sync.dma_start(w_stage[:, :, 0, :], by_quadrant(w_scales))
         nc.sync.dma_start(w_stage[:, :, 1, :], by_quadrant(w0_scales))
         xt_w = load_words("xt_w", xt_words[0], U16, T)
@@ -100,22 +100,22 @@ def tile_list_twotables_bank_one_pagetwice_kernel(
                 dealt[:].rearrange("p (t c m) -> p c t m", t=PACK, m=4), raw[:].rearrange("p (c m t) -> p c t m", t=PACK, m=4)
             )
 
-        def gather(name, window, offsets, dtype):
-            tile = sb.tile([P, HALF], dtype, name=name, align_bytes=64)
+        def gather(name, window, offsets, dtype, tag=None):
+            tile = sb.tile([P, HALF], dtype, name=name, tag=tag or name, align_bytes=64)
             nc.vector.tensor_copy(tile[:], window[:].indirect(offsets))
             return tile
 
         def half(tile, h):
             return tile[:, 8 * h : 8 * (h + 1)]
 
-        xt_gs0 = gather("xt_gs0", xt_s, half(l1, 0), U8)
-        xt_gw0 = gather("xt_gw0", xt_w, half(l1, 0), U16)
-
         spread(ws_raw, lambda q: w_stage[:, q, :, :].rearrange("p i c -> p (i c)"))
         ws_p = sb.tile([P, 2 * R], U8, name="ws_p", align_bytes=64)
         nc.vector.tensor_copy(
             ws_p[:].rearrange("p (i t m) -> p i t m", i=2, t=PACK), ws_raw[:].rearrange("p (i m t) -> p i t m", i=2, t=PACK)
         )
+
+        xt_gs0 = gather("xt_gs0", xt_s, half(l1, 0), U8)
+        xt_gw0 = gather("xt_gw0", xt_w, half(l1, 0), U16, "w_stage")
 
         for s in range(2):
             nc.vector.tensor_copy(xo_s[64 * s : 64 * (s + 1), :].bitcast(I32), xo_stage[64:P, s, :])
@@ -152,10 +152,13 @@ def tile_list_twotables_bank_one_pagetwice_kernel(
 
         sums0 = first_stage(0, xt_gw0, xt_gs0)
         xt_gs1 = gather("xt_gs1", xt_s, half(l1, 1), U8)
-        xt_gw1 = gather("xt_gw1", xt_w, half(l1, 1), U16)
+        xt_gw1 = gather("xt_gw1", xt_w, half(l1, 1), U16, "ws_raw")
         sums1 = first_stage(1, xt_gw1, xt_gs1)
+        for t in range(2, PACK):
+            nc.vector.tensor_copy(a_t[t][:, 0:HALF], sums0[t])
         for t in range(PACK):
-            nc.scalar.copy(a_t[t][:, 0:HALF], sums0[t])
+            if t < 2:
+                nc.scalar.copy(a_t[t][:, 0:HALF], sums0[t])
             look(g1[:, t, :], tb_t[t], l3, a_t[t][:, 0:1])
         for t in range(PACK):
             nc.vector.tensor_copy(a_t[t][:, HALF:J], sums1[t])

from contextlib import ExitStack

import concourse.mybir as mybir

FLOPS = 301989888

F32 = mybir.dt.float32
BF16 = mybir.dt.bfloat16
I32 = mybir.dt.int32
U32 = mybir.dt.uint32
U16 = mybir.dt.uint16
U8 = mybir.dt.uint8
E4M3 = mybir.dt.float8_e4m3fn_x4
E5M2 = mybir.dt.float8_e5m2_x4
E2M1 = mybir.dt.float4_e2m1fn_x4
COPY = mybir.ActivationFunctionType.Copy
ALU = mybir.AluOpType

P = 128
PACK = 4
QUADS = 4
T, J, R, X, O, N, E = 1024, 256, 512, 512, 128, 256, 512
HALF = J // 2


def tile_list_twotables_bank_one_pagetwice_kernel(
    tc, xt_words, xt_scales, xo_words, xo_scales, w_words, w_scales, w0_words, w0_scales,
    tb, tc2, wb_words, wb_scales, offs, offs2, offs3, offs4, offs5, offs6, offs7, out,
):
    nc = tc.nc
    with ExitStack() as ctx:
        sb = ctx.enter_context(tc.tile_pool(name="sb", bufs=1))
        ps = ctx.enter_context(tc.psum_pool(name="ps", bufs=1))

        def load_list(name, dram):
            tile = sb.tile(list(dram.shape), U16, name=name)
            nc.sync.dma_start(tile[:], dram)
            return tile

        def load_words(name, dram_bytes, dtype, columns):
            tile = sb.tile([P, columns], dtype, name=name, align_bytes=64)
            nc.sync.dma_start(tile[:].bitcast(I32), dram_bytes.bitcast(I32))
            return tile

        def by_quadrant(scales):
            return scales[0].bitcast(I32).rearrange("(q r) c -> r q c", r=PACK)

        def load_rows(name, dram, t):
            tile = sb.tile([P, X], F32, name=name)
            nc.sync.dma_start(tile[:], dram.rearrange("(p t) x -> t p x", t=PACK)[t])
            return tile

        xt_s = sb.tile([P, T], U8, name="xt_s")
        xo_s = sb.tile([P, T], U8, name="xo_s")
        ws_raw = sb.tile([P, 2 * R], U8, name="ws_raw", align_bytes=64)
        wb_s = sb.tile([P, N], U8, name="wb_s", align_bytes=64)
        xo_stage = sb.tile([P, 2, T // 4], I32, name="xo_stage")
        nc.gpsimd.memset(xo_stage[64:P], 0)
        for tile in (xt_s, ws_raw, wb_s):
            nc.vector.memset(tile[:].bitcast(I32), 0)

        l1 = load_list("l1", offs)
        xt_stage = sb.tile([PACK, QUADS, T // 4], I32, name="xt_stage")
        nc.sync.dma_start(xt_stage[:], by_quadrant(xt_scales))
        w_stage = sb.tile([PACK, QUADS, 2, R // 4], I32, name="w_stage", align_bytes=64)
        nc.sync.dma_start(w_stage[:, :, 0, :], by_quadrant(w_scales))
        nc.sync.dma_start(w_stage[:, :, 1, :], by_quadrant(w0_scales))
        xt_w = load_words("xt_w", xt_words[0], U16, T)
        w_raw = load_words("w_raw", w_words[0].rearrange("p n t -> p (n t)"), U32, R)
        w0_raw = load_words("w0_raw", w0_words[0].rearrange("p n t -> p (n t)"), U32, R)
        xo_w = load_words("xo_w", xo_words[0].rearrange("p n t -> p (n t)"), U32, T)
        xo_rows = xo_scales[0].bitcast(I32).rearrange("(s b r) c -> b r s c", s=2, r=PACK)
        for b in range(2):
            nc.sync.dma_start(xo_stage[64 + 32 * b : 64 + 32 * b + PACK], xo_rows[b])
        l2 = load_list("l2", offs2)
        tb_t = [load_rows("tb0", tb, 0)]
        l3 = load_list("l3", offs3)
        tb_t.extend(load_rows("tb%d" % t, tb, t) for t in range(1, PACK))
        l5 = load_list("l5", offs5)
        l4 = load_list("l4", offs4)
        tc_t = [load_rows("tc%d" % t, tc2, t) for t in range(PACK)]
        wb_w = load_words("wb_w", wb_words[0].rearrange("p n t -> p (n t)"), U32, N)
        for q in range(QUADS):
            nc.sync.dma_start(
                wb_s[32 * q : 32 * q + PACK, :].bitcast(I32), wb_scales[0, PACK * q : PACK * (q + 1), :].bitcast(I32)
            )
        l6 = load_list("l6", offs6)
        l7 = load_list("l7", offs7)

        def spread(plane, stage_of):
            for q in range(QUADS):
                nc.vector.tensor_copy(plane[32 * q : 32 * q + PACK, :].bitcast(I32), stage_of(q))

        spread(xt_s, lambda q: xt_stage[:, q, :])

        w_p = sb.tile([P, R], U32, name="w_p", align_bytes=64)
        w0_p = sb.tile([P, R], U32, name="w0_p", align_bytes=64)
        for dealt, raw in ((w_p, w_raw), (w0_p, w0_raw)):
            nc.scalar.copy(
                dealt[:].rearrange("p (t c m) -> p c t m", t=PACK, m=4), raw[:].rearrange("p (c m t) -> p c t m", t=PACK, m=4)
            )

        def gather(name, window, offsets, dtype, tag=None):
            tile = sb.tile([P, HALF], dtype, name=name, tag=tag or name, align_bytes=64)
            nc.vector.tensor_copy(tile[:], window[:].indirect(offsets))
            return tile

        def half(tile, h):
            return tile[:, 8 * h : 8 * (h + 1)]

        spread(ws_raw, lambda q: w_stage[:, q, :, :].rearrange("p i c -> p (i c)"))
        ws_p = sb.tile([P, 2 * R], U8, name="ws_p", align_bytes=64)
        nc.vector.tensor_copy(
            ws_p[:].rearrange("p (i t m) -> p i t m", i=2, t=PACK), ws_raw[:].rearrange("p (i m t) -> p i t m", i=2, t=PACK)
        )

        xt_gs0 = gather("xt_gs0", xt_s, half(l1, 0), U8)
        xt_gw0 = gather("xt_gw0", xt_w, half(l1, 0), U16, "w_stage")

        for s in range(2):
            nc.vector.tensor_copy(xo_s[64 * s : 64 * (s + 1), :].bitcast(I32), xo_stage[64:P, s, :])

        a_t = [sb.tile([P, J], F32, name="a%d" % t) for t in range(PACK)]

        def first_stage(h, xt_gw, xt_gs):
            xo_gw = gather("xo_gw%d" % h, xo_w, half(l2, h), U32)
            xo_gs = gather("xo_gs%d" % h, xo_s, half(l2, h), U8)
            banks = [ps.tile([P, 2, HALF], F32, name="a_ps%d%d" % (h, b)) for b in range(2)]
            for t in range(PACK):
                cols = slice(P * t, P * (t + 1))
                nc.tensor.matmul_mx(
                    banks[t // 2][:, t % 2, :], lhsT=w_p[:, cols].bitcast(E5M2), lhsT_scale=ws_p[:, cols],
                    rhs=xt_gw[:].bitcast(E2M1), rhs_scale=xt_gs[:], start=(t % 2 == 0), stop=False,
                )
            for t in range(PACK):
                cols = slice(P * t, P * (t + 1))
                nc.tensor.matmul_mx(
                    banks[t // 2][:, t % 2, :], lhsT=w0_p[:, cols].bitcast(E4M3),
                    lhsT_scale=ws_p[:, R + P * t : R + P * (t + 1)],
                    rhs=xo_gw[:].bitcast(E5M2), rhs_scale=xo_gs[:], start=False, stop=(t % 2 == 1),
                )
            return [banks[t // 2][:, t % 2, :] for t in range(PACK)]

        def look(product, table, offsets, scale):
            nc.scalar.activation(product, table[:].indirect(offsets[:]), COPY, scale=scale)

        g1 = sb.tile([P, PACK, O], F32, name="g1")
        g2 = sb.tile([P, PACK, O], F32, name="g2")
        a_g = sb.tile([P, PACK, O], F32, name="a_g")
        top = sb.tile([P, PACK, O], F32, name="top")
        hid = sb.tile([P, O, PACK], BF16, name="hid", align_bytes=64)

        sums0 = first_stage(0, xt_gw0, xt_gs0)
        xt_gs1 = gather("xt_gs1", xt_s, half(l1, 1), U8)
        xt_gw1 = gather("xt_gw1", xt_w, half(l1, 1), U16, "ws_raw")
        sums1 = first_stage(1, xt_gw1, xt_gs1)
        for t in range(2, PACK):
            nc.vector.tensor_copy(a_t[t][:, 0:HALF], sums0[t])
        for t in range(PACK):
            if t < 2:
                nc.scalar.copy(a_t[t][:, 0:HALF], sums0[t])
            look(g1[:, t, :], tb_t[t], l3, a_t[t][:, 0:1])
        for t in range(PACK):
            nc.vector.tensor_copy(a_t[t][:, HALF:J], sums1[t])
        for t in range(PACK):
            nc.vector.tensor_copy(a_g[:, t, :], a_t[t][:].indirect(l5[:]))
        for t in range(PACK):
            look(g2[:, t, :], tc_t[t], l4, a_t[t][:, HALF : HALF + 1])

        def larger(ts):
            nc.vector.tensor_tensor(top[:, ts, :], g1[:, ts, :], g2[:, ts, :], ALU.max)

        larger(slice(0, 2))
        larger(slice(2, 3))
        larger(slice(3, 4))
        nc.vector.tensor_tensor(
            hid[:].rearrange("p (c i) t -> p c t i", i=4),
            top[:].rearrange("p t (c i) -> p c t i", i=4),
            a_g[:].rearrange("p t (c i) -> p c t i", i=4),
            ALU.subtract,
        )

        pa = [sb.tile([P, E], F32, name="pa%d" % h, tag=("ws_p", "xo_w")[h], align_bytes=64) for h in range(2)]
        pb = [sb.tile([P, E], F32, name="pb%d" % h, tag=("w_p", "w0_p")[h], align_bytes=64) for h in range(2)]
        for tile in pa + pb:
            nc.gpsimd.memset(tile[:], 0.0)

        hid_w = sb.tile([P, O], U32, name="hid_w", align_bytes=64)
        hid_s = sb.tile([P, O], U8, name="hid_s", align_bytes=64)
        nc.vector.quantize_mx(hid_w[:].bitcast(E5M2), hid_s[:], hid[:].rearrange("p o t -> p (o t)"))

        p_sb = []
        for h in range(2):
            cols = slice(P * h, P * (h + 1))
            bank = ps.tile([P, O], F32, name="p_ps%d" % h)
            nc.tensor.matmul_mx(
                bank[:], lhsT=wb_w[:, cols].bitcast(E4M3), lhsT_scale=wb_s[:, cols],
                rhs=hid_w[:].bitcast(E5M2), rhs_scale=hid_s[:], start=True, stop=True,
            )
            tile = sb.tile([P, O], F32, name="p_sb%d" % h)
            if h == 0:
                nc.vector.tensor_copy(tile[:], bank[:])
            else:
                nc.scalar.copy(tile[:], bank[:])
            p_sb.append(tile)
        for h in range(2):
            nc.vector.tensor_copy(pa[h][:].indirect(l6[:]), p_sb[h][:])
            nc.scalar.activation(pb[h][:].indirect(l7[:]), p_sb[h][:], COPY)
        for h, cuts in enumerate(((0, E), (0, E // 2, E))):
            total = sb.tile([P, E], F32, name="total%d" % h)
            for lo, hi in zip(cuts, cuts[1:]):
                nc.vector.tensor_tensor(total[:, lo:hi], pa[h][:, lo:hi], pb[h][:, lo:hi], ALU.add)
                nc.sync.dma_start(out[P * h : P * (h + 1), lo:hi], total[:, lo:hi])
